import numpy as np
import ml_dtypes


def mxq(x, axis, fmt="e4m3"):
    dtype, down = {"e4m3": (ml_dtypes.float8_e4m3fn, 7), "e5m2": (ml_dtypes.float8_e5m2, 14)}[fmt]
    v = np.moveaxis(np.asarray(x, np.float32).astype(ml_dtypes.bfloat16).astype(np.float64), axis, -1)
    blocks = v.reshape(v.shape[:-1] + (-1, 32))
    amax = np.abs(blocks).max(-1, keepdims=True)
    byte = np.maximum(np.where(amax > 0, np.frexp(amax)[1] - 1 + 127, 0) - down, 1)
    scale = np.exp2(byte - 127.0)
    codes = (blocks / scale).astype(np.float32).astype(dtype).astype(np.float64)
    return np.moveaxis((codes * scale).reshape(v.shape), -1, axis)


WIDE = False


def mx_kscale(k):
    if not WIDE:
        return np.ones(k)
    levels = np.array([10, -10, 5, -5, 0])
    if k % 512:
        return np.exp2(np.random.permutation(np.resize(levels, k // 32))).repeat(32)
    a = np.empty((k // 512, 16))
    for p in range(k // 512):
        a[p, :8] = np.random.permutation(np.resize(levels, 8))
        for g in range(8):
            far = levels[np.abs(levels - a[p, g]) >= 10]
            a[p, g + 8] = far[np.random.randint(len(far))]
    return np.exp2(a.ravel()).repeat(32)


def f64(x):
    return np.asarray(x).astype(np.float64)


def striped(idx):
    return np.tile(idx.reshape(-1, 16).T, (8, 1)).astype(np.uint16)


def unstriped(offs):
    return offs[:16].T.reshape(-1).astype(np.int64)


def pack_weight(w):
    k, n = w.shape
    w = f64(np.asarray(w, np.float32).astype(ml_dtypes.bfloat16)).reshape(k // 32, 32, n)
    amax = np.abs(w).max(1)
    byte = np.clip(np.where(amax > 0, np.frexp(amax)[1] - 1 + 127 - 7, 1), 1, 254)
    scaled = (w * np.exp2(127.0 - byte)[:, None, :]).reshape(k, n).astype(np.float32)
    words = np.ascontiguousarray(scaled.reshape(k // 512, 128, 4, n).transpose(0, 1, 3, 2)).astype(ml_dtypes.float8_e4m3fn).view(np.uint8)
    return words, np.ascontiguousarray(byte.astype(np.uint8).reshape(k // 512, 16, n))


def unpack_weight(words, scales):
    g, p, n, _ = words.shape
    vals = np.ascontiguousarray(words).view(ml_dtypes.float8_e4m3fn).astype(np.float64) * np.repeat(np.exp2(scales.astype(np.float64) - 127.0), 8, axis=1)[..., None]
    return vals.transpose(0, 1, 3, 2).reshape(g * 512, n)


K, T, E, C, N = 1536, 512, 8, 256, 256
TOP = 4


def by_expert(wq, xq):
    return np.concatenate([wq[e].T @ xq[:, e * C:(e + 1) * C] for e in range(E)], axis=1)


def setup_inputs():
    n = np.random.standard_normal
    s = mx_kscale(K)[:, None]
    deal = np.repeat(np.arange(E), C).reshape(TOP, T)[:, np.random.permutation(T)]
    deal = np.take_along_axis(deal, np.argsort(np.random.rand(TOP, T), axis=0), axis=0)
    for _ in range(8):
        s_, t_ = np.random.permutation(T).reshape(2, -1); r = np.random.randint(TOP, size=T // 2); x, y = deal[r, s_].copy(), deal[r, t_].copy()
        ok = ~((deal[:, s_] == y).any(0) | (deal[:, t_] == x).any(0)); deal[r[ok], s_[ok]] = y[ok]; deal[r[ok], t_[ok]] = x[ok]
    order = np.lexsort((np.random.rand(TOP * T), deal.reshape(-1)))
    slot_token = order % T; pos = np.empty(TOP * T, np.int64); pos[order] = np.arange(TOP * T); pos = pos.reshape(TOP, T)
    g = np.random.uniform(0.5, 1.5, (TOP, T)); g = g / g.sum(0)
    packed = [pack_weight(m) for m in n((E, K, N)) / np.sqrt(K) / s[None]]
    w_slot = np.empty(E * C)
    for r in range(TOP): w_slot[pos[r]] = g[r]
    return {
        "xT": (n((K, T)) * s).astype(np.float32),
        "w_words": np.stack([m[0] for m in packed]),
        "w_scales": np.stack([m[1] for m in packed]),
        "b": (0.3 * n((N, E))).astype(np.float32),
        "gate": np.tile(w_slot, (K, 1)).astype(np.float32),
        "offs": striped(slot_token),
        "pos1": striped(pos[0]),
        "pos2": striped(pos[1]),
        "pos3": striped(pos[2]),
        "pos4": striped(pos[3]),
    }


def reference(xT, w_words, w_scales, b, gate, offs, pos1, pos2, pos3, pos4):
    idx = unstriped(offs)
    w = np.stack([unpack_weight(w_words[e], w_scales[e]) for e in range(E)])
    xq = mxq(f64(gate) * f64(xT)[:, idx], 0, "e4m3")
    y = by_expert(w, xq)
    y = y + np.repeat(f64(b), C, axis=1)
    return y[:, unstriped(pos1)] + y[:, unstriped(pos2)] + y[:, unstriped(pos3)] + y[:, unstriped(pos4)]

@@ -1,0 +1,162 @@
+from contextlib import ExitStack
+
+import concourse.mybir as mybir
+
+K, T, E, C, N = 1536, 512, 8, 256, 256
+TOP = 4
+S = E * C
+P = 128
+PACK = 4
+PASSES = K // (P * PACK)
+HALVES = N // P
+PAD = 8
+PER_COL = 16
+
+F32 = mybir.dt.float32
+BF16 = mybir.dt.bfloat16
+I32 = mybir.dt.int32
+U32 = mybir.dt.uint32
+U16 = mybir.dt.uint16
+U8 = mybir.dt.uint8
+FP8X4 = mybir.dt.float8_e4m3fn_x4
+MULT = mybir.AluOpType.mult
+ADD = mybir.AluOpType.add
+IDENTITY = mybir.ActivationFunctionType.Identity
+
+FLOPS = 2 * K * N * S
+BYTES = 4 * K * T + E * K * N + E * K * N // 32 + 4 * N * E + 4 * S + 2 * P * (S + TOP * T) // PER_COL + 4 * N * T
+
+CHUNKS = [(0, 512), (512, 512), (1024, 512), (1536, 256), (1792, 256)]
+FIRST_GATE = 128
+LAG = 2
+
+
+def tile_moe_pre_lin_bias_kernel(tc, xT, w_words, w_scales, b, gate, offs, pos1, pos2, pos3, pos4, out):
+    nc = tc.nc
+    with ExitStack() as ctx:
+        keep = ctx.enter_context(tc.tile_pool(name="keep", bufs=1))
+        stage = ctx.enter_context(tc.tile_pool(name="stage", bufs=4))
+        psum = ctx.enter_context(tc.psum_pool(name="psum", bufs=8))
+
+        offs_sb = keep.tile([P, S // PER_COL], U16, name="offs_sb")
+        pos_sb = [keep.tile([P, T // PER_COL], U16, name="pos%d" % r) for r in range(TOP)]
+        rows = [[keep.tile([P, T + PAD], F32, name="rows%d_%d" % (a, j)) for j in range(PACK)] for a in range(PASSES)]
+        gate_sb = keep.tile([P, S], F32, name="gate_sb")
+        w_sb = [keep.tile([P, PASSES, N], U32, name="w%d" % e, align_bytes=64) for e in range(E)]
+        w_sc = keep.tile([P, E * PASSES, N], U8, name="w_sc", align_bytes=64)
+        bias = keep.tile([P, HALVES, E], F32, name="bias")
+        x_codes = [keep.tile([P, S], U32, name="x_codes%d" % a, align_bytes=64) for a in range(PASSES)]
+        x_sc = [keep.tile([P, S], U8, name="x_sc%d" % a, align_bytes=64) for a in range(PASSES)]
+        y = [keep.tile([P, S], F32, name="y%d" % h) for h in range(HALVES)]
+
+        for a in range(PASSES):
+            for j in range(PACK):
+                nc.vector.memset(rows[a][j][:, T:], 0.0)
+        nc.vector.memset(w_sc[:].rearrange("p g n -> p (g n)").bitcast(I32), 0)
+
+        def load_rows(a, j):
+            src = xT[a * P * PACK:(a + 1) * P * PACK, :].rearrange("(p j) t -> p j t", j=PACK)
+            nc.sync.dma_start(out=rows[a][j][:, :T], in_=src[:, j, :])
+
+        def load_gate(s0, s1):
+            nc.sync.dma_start(out=gate_sb[:, s0:s1], in_=gate[0:P, s0:s1])
+
+        def load_weights(e):
+            nc.sync.dma_start(out=w_sb[e][:].bitcast(I32), in_=w_words[e].rearrange("a p n r -> p a (n r)").bitcast(I32))
+
+        nc.sync.dma_start(offs_sb[:], offs)
+        load_rows(0, 0)
+        load_gate(0, FIRST_GATE)
+        load_gate(FIRST_GATE, CHUNKS[0][1])
+        for a in range(PASSES):
+            for j in range(PACK):
+                if (a, j) != (0, 0):
+                    load_rows(a, j)
+        load_gate(CHUNKS[0][1], 2 * CHUNKS[0][1])
+        scale_rows = w_scales.rearrange("e a q n -> q (e a) n").bitcast(I32)
+        for quad in range(4):
+            nc.sync.dma_start(out=w_sc[32 * quad:32 * quad + 4, :, :].bitcast(I32), in_=scale_rows[4 * quad:4 * quad + 4, :, :])
+        load_weights(0)
+        load_weights(1)
+        nc.sync.dma_start(out=bias[:], in_=b.rearrange("(h p) e -> p h e", p=P))
+        load_gate(2 * CHUNKS[0][1], S)
+        for e in range(2, E):
+            load_weights(e)
+        for r, pos in enumerate((pos1, pos2, pos3, pos4)):
+            nc.sync.dma_start(pos_sb[r][:], pos)
+
+        pieces = [(s0, n, a) for s0, n in CHUNKS for a in range(PASSES)]
+        s_last, n_last, a_last = pieces.pop()
+        pieces += [(s_last, n_last // 2, a_last), (s_last + n_last // 2, n_last // 2, a_last)]
+        groups = [(e * C, C) for e in range(E - 1)] + [(s_last, n_last // 2), (s_last + n_last // 2, n_last // 2)]
+        acc = {}
+
+        def gather(s0, n, a):
+            picked = stage.tile([P, PACK, n], F32, name="picked")
+            for j in range(PACK):
+                cuts = [0, FIRST_GATE, n] if (s0, a, j) == (0, 0, 0) else [0, n]
+                for c0, c1 in zip(cuts, cuts[1:]):
+                    window = rows[a][j][:].indirect(offs_sb[:, (s0 + c0) // PER_COL:(s0 + c1) // PER_COL])
+                    nc.vector.tensor_tensor(picked[:, j, c0:c1], window, gate_sb[:, s0 + c0:s0 + c1], MULT)
+            rounded = stage.tile([P, n, PACK], BF16, name="rounded", align_bytes=64)
+            nc.scalar.copy(out=rounded[:], in_=picked[:].rearrange("p j c -> p c j"))
+            return rounded
+
+        def multiply(s0, n, a, rounded):
+            nc.vector.quantize_mx(
+                out=x_codes[a][:, s0:s0 + n].bitcast(FP8X4),
+                scales=x_sc[a][:, s0:s0 + n],
+                in_=rounded[:].rearrange("p c j -> p (c j)"),
+            )
+            for g0, width in groups:
+                if s0 <= g0 < s0 + n:
+                    e = g0 // C
+                    for h in range(HALVES):
+                        if a == 0:
+                            acc[g0, h] = psum.tile([P, width], F32, name="acc")
+                        nc.tensor.matmul_mx(
+                            out=acc[g0, h][:],
+                            lhsT=w_sb[e][:, a, h * P:(h + 1) * P].bitcast(FP8X4),
+                            lhsT_scale=w_sc[:, e * PASSES + a, h * P:(h + 1) * P],
+                            rhs=x_codes[a][:, g0:g0 + width].bitcast(FP8X4),
+                            rhs_scale=x_sc[a][:, g0:g0 + width],
+                            start=(a == 0),
+                            stop=(a == PASSES - 1),
+                        )
+                        if a == PASSES - 1:
+                            nc.scalar.activation(y[h][:, g0:g0 + width], acc[g0, h][:], IDENTITY, bias=bias[:, h, e:e + 1])
+
+        waiting = []
+        for piece in pieces:
+            waiting.append(piece + (gather(*piece),))
+            if len(waiting) > LAG:
+                multiply(*waiting.pop(0))
+        for item in waiting:
+            multiply(*item)
+
+        back = [keep.tile([P, TOP, T], F32, name="back%d" % h) for h in range(HALVES)]
+        part = [keep.tile([P, 2, T], F32, name="part%d" % h) for h in range(HALVES)]
+        total = [keep.tile([P, T], F32, name="total%d" % h) for h in range(HALVES)]
+
+        def fetch(h, r, t0, t1):
+            nc.vector.tensor_copy(back[h][:, r, t0:t1], y[h][:].indirect(pos_sb[r][:, t0 // PER_COL:t1 // PER_COL]))
+
+        def store(h, t0, t1):
+            nc.sync.dma_start(out=out[h * P:(h + 1) * P, t0:t1], in_=total[h][:, t0:t1])
+
+        for r in range(TOP):
+            fetch(0, r, 0, T)
+        fetch(1, 0, 0, T)
+        nc.vector.tensor_tensor(part[0][:], back[0][:, 0:2, :], back[0][:, 2:4, :], ADD)
+        fetch(1, 1, 0, T)
+        nc.vector.tensor_tensor(total[0][:], part[0][:, 0, :], part[0][:, 1, :], ADD)
+        store(0, 0, T)
+        fetch(1, 2, 0, T)
+        nc.vector.tensor_tensor(part[1][:, 0, :], back[1][:, 0, :], back[1][:, 1, :], ADD)
+        fetch(1, 3, 0, T // 2)
+        nc.vector.tensor_tensor(part[1][:, 1, :], part[1][:, 0, :], back[1][:, 2, :], ADD)
+        fetch(1, 3, T // 2, T)
+        for t0 in (0, T // 2):
+            t1 = t0 + T // 2
+            nc.vector.tensor_tensor(total[1][:, t0:t1], part[1][:, 1, t0:t1], back[1][:, 3, t0:t1], ADD)
+            store(1, t0, t1)

@@ -1,6 +1,7 @@
 from contextlib import ExitStack
 
 import concourse.mybir as mybir
+from concourse.masks import make_identity
 
 K, T, E, C, N = 1536, 512, 8, 256, 256
 TOP = 4
@@ -9,7 +10,7 @@ P = 128
 PACK = 4
 PASSES = K // (P * PACK)
 HALVES = N // P
-PAD = 8
+WINDOW = 1032
 PER_COL = 16
 
 F32 = mybir.dt.float32
@@ -26,21 +27,26 @@ IDENTITY = mybir.ActivationFunctionType.Identity
 FLOPS = 2 * K * N * S
 BYTES = 4 * K * T + E * K * N + E * K * N // 32 + 4 * N * E + 4 * S + 2 * P * (S + TOP * T) // PER_COL + 4 * N * T
 
-CHUNKS = [(0, 512), (512, 512), (1024, 512), (1536, 256), (1792, 256)]
-FIRST_GATE = 128
-LAG = 2
+PIECES = [(0, 1024, 0), (0, 1024, 1), (0, 1024, 2), (1024, 512, 0), (1024, 512, 1), (1024, 512, 2),
+          (1536, 512, 0), (1536, 512, 1), (1536, 256, 2), (1792, 128, 2), (1920, 128, 2)]
+HELD = 3
+UNIT = 256
+GATE_CUTS = [0, 128, 512, 1024, 2048]
+QUANT = 512
+LINE = 4
 
 
 def tile_moe_pre_lin_bias_kernel(tc, xT, w_words, w_scales, b, gate, offs, pos1, pos2, pos3, pos4, out):
     nc = tc.nc
     with ExitStack() as ctx:
         keep = ctx.enter_context(tc.tile_pool(name="keep", bufs=1))
-        stage = ctx.enter_context(tc.tile_pool(name="stage", bufs=4))
+        stage = ctx.enter_context(tc.tile_pool(name="stage", bufs=2))
+        narrow = ctx.enter_context(tc.tile_pool(name="narrow", bufs=6))
         psum = ctx.enter_context(tc.psum_pool(name="psum", bufs=8))
 
         offs_sb = keep.tile([P, S // PER_COL], U16, name="offs_sb")
         pos_sb = [keep.tile([P, T // PER_COL], U16, name="pos%d" % r) for r in range(TOP)]
-        rows = [[keep.tile([P, T + PAD], F32, name="rows%d_%d" % (a, j)) for j in range(PACK)] for a in range(PASSES)]
+        rows = [[keep.tile([P, WINDOW], F32, name="rows%d_%d" % (a, j)) for j in range(PACK)] for a in range(PASSES)]
         gate_sb = keep.tile([P, S], F32, name="gate_sb")
         w_sb = [keep.tile([P, PASSES, N], U32, name="w%d" % e, align_bytes=64) for e in range(E)]
         w_sc = keep.tile([P, E * PASSES, N], U8, name="w_sc", align_bytes=64)
@@ -49,9 +55,8 @@ def tile_moe_pre_lin_bias_kernel(tc, xT, w_words, w_scales, b, gate, offs, pos1,
         x_sc = [keep.tile([P, S], U8, name="x_sc%d" % a, align_bytes=64) for a in range(PASSES)]
         y = [keep.tile([P, S], F32, name="y%d" % h) for h in range(HALVES)]
 
-        for a in range(PASSES):
-            for j in range(PACK):
-                nc.vector.memset(rows[a][j][:, T:], 0.0)
+        ident = keep.tile([P, P], F32, name="ident")
+        make_identity(nc, ident[:])
         nc.vector.memset(w_sc[:].rearrange("p g n -> p (g n)").bitcast(I32), 0)
 
         def load_rows(a, j):
@@ -66,97 +71,126 @@ def tile_moe_pre_lin_bias_kernel(tc, xT, w_words, w_scales, b, gate, offs, pos1,
 
         nc.sync.dma_start(offs_sb[:], offs)
         load_rows(0, 0)
-        load_gate(0, FIRST_GATE)
-        load_gate(FIRST_GATE, CHUNKS[0][1])
+        for g0, g1 in zip(GATE_CUTS[:3], GATE_CUTS[1:4]):
+            load_gate(g0, g1)
         for a in range(PASSES):
             for j in range(PACK):
                 if (a, j) != (0, 0):
                     load_rows(a, j)
-        load_gate(CHUNKS[0][1], 2 * CHUNKS[0][1])
         scale_rows = w_scales.rearrange("e a q n -> q (e a) n").bitcast(I32)
         for quad in range(4):
             nc.sync.dma_start(out=w_sc[32 * quad:32 * quad + 4, :, :].bitcast(I32), in_=scale_rows[4 * quad:4 * quad + 4, :, :])
         load_weights(0)
         load_weights(1)
         nc.sync.dma_start(out=bias[:], in_=b.rearrange("(h p) e -> p h e", p=P))
-        load_gate(2 * CHUNKS[0][1], S)
+        load_gate(GATE_CUTS[3], S)
         for e in range(2, E):
             load_weights(e)
         for r, pos in enumerate((pos1, pos2, pos3, pos4)):
             nc.sync.dma_start(pos_sb[r][:], pos)
 
-        pieces = [(s0, n, a) for s0, n in CHUNKS for a in range(PASSES)]
-        s_last, n_last, a_last = pieces.pop()
-        pieces += [(s_last, n_last // 2, a_last), (s_last + n_last // 2, n_last // 2, a_last)]
-        groups = [(e * C, C) for e in range(E - 1)] + [(s_last, n_last // 2), (s_last + n_last // 2, n_last // 2)]
+        groups = [(e * C, C) for e in range(E - 1)] + [(S - C, C // 2), (S - C // 2, C // 2)]
         acc = {}
 
         def gather(s0, n, a):
             picked = stage.tile([P, PACK, n], F32, name="picked")
             for j in range(PACK):
-                cuts = [0, FIRST_GATE, n] if (s0, a, j) == (0, 0, 0) else [0, n]
+                cuts = GATE_CUTS[:4] if (s0, a, j) == (0, 0, 0) else [0, n]
                 for c0, c1 in zip(cuts, cuts[1:]):
                     window = rows[a][j][:].indirect(offs_sb[:, (s0 + c0) // PER_COL:(s0 + c1) // PER_COL])
                     nc.vector.tensor_tensor(picked[:, j, c0:c1], window, gate_sb[:, s0 + c0:s0 + c1], MULT)
-            rounded = stage.tile([P, n, PACK], BF16, name="rounded", align_bytes=64)
-            nc.scalar.copy(out=rounded[:], in_=picked[:].rearrange("p j c -> p c j"))
-            return rounded
+            made = []
+            for c0 in range(0, n, QUANT):
+                m = min(QUANT, n)
+                rounded = narrow.tile([P, m, PACK], BF16, name="rounded", align_bytes=64)
+                dst = rounded[:].rearrange("p (c i) j -> p c j i", i=LINE)
+                src = picked[:, :, c0:c0 + m].rearrange("p j (c i) -> p c j i", i=LINE)
+                nc.scalar.copy(out=dst, in_=src)
+                made.append((s0 + c0, m, a, rounded))
+            return made
 
-        def multiply(s0, n, a, rounded):
+        def quantize(s0, n, a, rounded):
             nc.vector.quantize_mx(
                 out=x_codes[a][:, s0:s0 + n].bitcast(FP8X4),
                 scales=x_sc[a][:, s0:s0 + n],
                 in_=rounded[:].rearrange("p c j -> p (c j)"),
             )
+
+        def multiply(s0, n, a, h):
             for g0, width in groups:
                 if s0 <= g0 < s0 + n:
                     e = g0 // C
-                    for h in range(HALVES):
-                        if a == 0:
-                            acc[g0, h] = psum.tile([P, width], F32, name="acc")
-                        nc.tensor.matmul_mx(
-                            out=acc[g0, h][:],
-                            lhsT=w_sb[e][:, a, h * P:(h + 1) * P].bitcast(FP8X4),
-                            lhsT_scale=w_sc[:, e * PASSES + a, h * P:(h + 1) * P],
-                            rhs=x_codes[a][:, g0:g0 + width].bitcast(FP8X4),
-                            rhs_scale=x_sc[a][:, g0:g0 + width],
-                            start=(a == 0),
-                            stop=(a == PASSES - 1),
-                        )
-                        if a == PASSES - 1:
+                    if a == 0:
+                        acc[g0, h] = psum.tile([P, width], F32, name="bank")
+                    nc.tensor.matmul_mx(
+                        out=acc[g0, h][:],
+                        lhsT=w_sb[e][:, a, h * P:(h + 1) * P].bitcast(FP8X4),
+                        lhsT_scale=w_sc[:, e * PASSES + a, h * P:(h + 1) * P],
+                        rhs=x_codes[a][:, g0:g0 + width].bitcast(FP8X4),
+                        rhs_scale=x_sc[a][:, g0:g0 + width],
+                        start=(a == 0),
+                        stop=(a == PASSES - 1),
+                    )
+                    if a == PASSES - 1:
+                        if (g0, h) == (groups[-1][0], 0):
+                            nc.vector.tensor_scalar(y[h][:, g0:g0 + width], acc[g0, h][:], bias[:, h, e:e + 1], None, ADD)
+                        else:
                             nc.scalar.activation(y[h][:, g0:g0 + width], acc[g0, h][:], IDENTITY, bias=bias[:, h, e:e + 1])
 
         waiting = []
-        for piece in pieces:
-            waiting.append(piece + (gather(*piece),))
-            if len(waiting) > LAG:
-                multiply(*waiting.pop(0))
-        for item in waiting:
-            multiply(*item)
+        for i, piece in enumerate(PIECES):
+            made = gather(*piece)
+            if i <= len(PIECES) - HELD:
+                for s0, n, a, rounded in waiting:
+                    quantize(s0, n, a, rounded)
+                    for h in range(HALVES):
+                        multiply(s0, n, a, h)
+                waiting = []
+            waiting += made
+        for s0, n, a, rounded in waiting:
+            quantize(s0, n, a, rounded)
+            multiply(s0, n, a, 0)
+        for s0, n, a, rounded in waiting:
+            multiply(s0, n, a, 1)
 
         back = [keep.tile([P, TOP, T], F32, name="back%d" % h) for h in range(HALVES)]
-        part = [keep.tile([P, 2, T], F32, name="part%d" % h) for h in range(HALVES)]
-        total = [keep.tile([P, T], F32, name="total%d" % h) for h in range(HALVES)]
 
         def fetch(h, r, t0, t1):
             nc.vector.tensor_copy(back[h][:, r, t0:t1], y[h][:].indirect(pos_sb[r][:, t0 // PER_COL:t1 // PER_COL]))
 
-        def store(h, t0, t1):
-            nc.sync.dma_start(out=out[h * P:(h + 1) * P, t0:t1], in_=total[h][:, t0:t1])
+        def store(queue, h, t0, total):
+            queue.dma_start(out=out[h * P:(h + 1) * P, t0:t0 + UNIT], in_=total[:])
 
-        for r in range(TOP):
-            fetch(0, r, 0, T)
-        fetch(1, 0, 0, T)
-        nc.vector.tensor_tensor(part[0][:], back[0][:, 0:2, :], back[0][:, 2:4, :], ADD)
-        fetch(1, 1, 0, T)
-        nc.vector.tensor_tensor(total[0][:], part[0][:, 0, :], part[0][:, 1, :], ADD)
-        store(0, 0, T)
-        fetch(1, 2, 0, T)
-        nc.vector.tensor_tensor(part[1][:, 0, :], back[1][:, 0, :], back[1][:, 1, :], ADD)
-        fetch(1, 3, 0, T // 2)
-        nc.vector.tensor_tensor(part[1][:, 1, :], part[1][:, 0, :], back[1][:, 2, :], ADD)
-        fetch(1, 3, T // 2, T)
-        for t0 in (0, T // 2):
-            t1 = t0 + T // 2
-            nc.vector.tensor_tensor(total[1][:, t0:t1], part[1][:, 1, t0:t1], back[1][:, 3, t0:t1], ADD)
-            store(1, t0, t1)
+        def turn_and_add(turned, h, r, t0):
+            for c0 in range(0, UNIT, P):
+                nc.tensor.matmul(turned[:, c0:c0 + P], lhsT=back[h][:, r, t0 + c0:t0 + c0 + P], rhs=ident[:],
+                                 start=(r == 0 and c0 == 0), stop=(r == TOP - 1 and c0 == UNIT - P), is_transpose=True)
+
+        def turn_back(turned, h, t0):
+            summed = narrow.tile([P, UNIT], F32, name="summed")
+            nc.scalar.copy(out=summed[:], in_=turned[:])
+            upright = psum.tile([P, UNIT], F32, name="bank")
+            for c0 in range(0, UNIT, P):
+                nc.tensor.transpose(upright[:, c0:c0 + P], summed[:, c0:c0 + P], ident[:])
+            total = narrow.tile([P, UNIT], F32, name="total")
+            nc.scalar.copy(out=total[:], in_=upright[:])
+            store(nc.scalar, h, t0, total)
+
+        for h, t0, t1 in ((0, 0, T), (1, 0, UNIT)):
+            turned = {u: psum.tile([P, UNIT], F32, name="bank") for u in range(t0, t1, UNIT)}
+            for r in range(TOP):
+                fetch(h, r, t0, t1)
+                for u in range(t0, t1, UNIT):
+                    turn_and_add(turned[u], h, r, u)
+            for u in range(t0, t1, UNIT):
+                turn_back(turned[u], h, u)
+        two = keep.tile([P, UNIT], F32, name="two")
+        three = keep.tile([P, UNIT], F32, name="three")
+        four = keep.tile([P, UNIT], F32, name="four")
+        for r in range(TOP - 1):
+            fetch(1, r, UNIT, T)
+        nc.vector.tensor_tensor(two[:], back[1][:, 0, UNIT:], back[1][:, 1, UNIT:], ADD)
+        fetch(1, TOP - 1, UNIT, T)
+        nc.vector.tensor_tensor(three[:], two[:], back[1][:, 2, UNIT:], ADD)
+        nc.vector.tensor_tensor(four[:], three[:], back[1][:, 3, UNIT:], ADD)
+        store(nc.sync, 1, UNIT, four)

@@ -27,12 +27,11 @@ IDENTITY = mybir.ActivationFunctionType.Identity
 FLOPS = 2 * K * N * S
 BYTES = 4 * K * T + E * K * N + E * K * N // 32 + 4 * N * E + 4 * S + 2 * P * (S + TOP * T) // PER_COL + 4 * N * T
 
-PIECES = [(0, 1024, 0), (0, 1024, 1), (0, 1024, 2), (1024, 512, 0), (1024, 512, 1), (1024, 512, 2),
-          (1536, 512, 0), (1536, 512, 1), (1536, 256, 2), (1792, 128, 2), (1920, 128, 2)]
+PIECES = [(0, 1024, 0), (0, 1024, 1), (0, 1024, 2), (1024, 1024, 0), (1024, 1024, 1),
+          (1024, 512, 2), (1536, 256, 2), (1792, 128, 2), (1920, 128, 2)]
 HELD = 3
 UNIT = 256
 GATE_CUTS = [0, 128, 512, 1024, 2048]
-QUANT = 512
 LINE = 4
 
 
@@ -41,7 +40,7 @@ def tile_moe_pre_lin_bias_kernel(tc, xT, w_words, w_scales, b, gate, offs, pos1,
     with ExitStack() as ctx:
         keep = ctx.enter_context(tc.tile_pool(name="keep", bufs=1))
         stage = ctx.enter_context(tc.tile_pool(name="stage", bufs=2))
-        narrow = ctx.enter_context(tc.tile_pool(name="narrow", bufs=6))
+        narrow = ctx.enter_context(tc.tile_pool(name="narrow", bufs=4))
         psum = ctx.enter_context(tc.psum_pool(name="psum", bufs=8))
 
         offs_sb = keep.tile([P, S // PER_COL], U16, name="offs_sb")
@@ -77,14 +76,12 @@ def tile_moe_pre_lin_bias_kernel(tc, xT, w_words, w_scales, b, gate, offs, pos1,
             for j in range(PACK):
                 if (a, j) != (0, 0):
                     load_rows(a, j)
+        load_gate(GATE_CUTS[3], S)
         scale_rows = w_scales.rearrange("e a q n -> q (e a) n").bitcast(I32)
         for quad in range(4):
             nc.sync.dma_start(out=w_sc[32 * quad:32 * quad + 4, :, :].bitcast(I32), in_=scale_rows[4 * quad:4 * quad + 4, :, :])
-        load_weights(0)
-        load_weights(1)
         nc.sync.dma_start(out=bias[:], in_=b.rearrange("(h p) e -> p h e", p=P))
-        load_gate(GATE_CUTS[3], S)
-        for e in range(2, E):
+        for e in range(E):
             load_weights(e)
         for r, pos in enumerate((pos1, pos2, pos3, pos4)):
             nc.sync.dma_start(pos_sb[r][:], pos)
@@ -99,15 +96,10 @@ def tile_moe_pre_lin_bias_kernel(tc, xT, w_words, w_scales, b, gate, offs, pos1,
                 for c0, c1 in zip(cuts, cuts[1:]):
                     window = rows[a][j][:].indirect(offs_sb[:, (s0 + c0) // PER_COL:(s0 + c1) // PER_COL])
                     nc.vector.tensor_tensor(picked[:, j, c0:c1], window, gate_sb[:, s0 + c0:s0 + c1], MULT)
-            made = []
-            for c0 in range(0, n, QUANT):
-                m = min(QUANT, n)
-                rounded = narrow.tile([P, m, PACK], BF16, name="rounded", align_bytes=64)
-                dst = rounded[:].rearrange("p (c i) j -> p c j i", i=LINE)
-                src = picked[:, :, c0:c0 + m].rearrange("p j (c i) -> p c j i", i=LINE)
-                nc.scalar.copy(out=dst, in_=src)
-                made.append((s0 + c0, m, a, rounded))
-            return made
+            rounded = narrow.tile([P, n, PACK], BF16, name="rounded", align_bytes=64)
+            nc.scalar.copy(out=rounded[:].rearrange("p (c i) j -> p c j i", i=LINE),
+                           in_=picked[:].rearrange("p j (c i) -> p c j i", i=LINE))
+            return rounded
 
         def quantize(s0, n, a, rounded):
             nc.vector.quantize_mx(
@@ -116,42 +108,54 @@ def tile_moe_pre_lin_bias_kernel(tc, xT, w_words, w_scales, b, gate, offs, pos1,
                 in_=rounded[:].rearrange("p c j -> p (c j)"),
             )
 
-        def multiply(s0, n, a, h):
+        def one_pass(bank, g0, width, a, h):
+            e = g0 // C
+            nc.tensor.matmul_mx(
+                out=bank[:],
+                lhsT=w_sb[e][:, a, h * P:(h + 1) * P].bitcast(FP8X4),
+                lhsT_scale=w_sc[:, e * PASSES + a, h * P:(h + 1) * P],
+                rhs=x_codes[a][:, g0:g0 + width].bitcast(FP8X4),
+                rhs_scale=x_sc[a][:, g0:g0 + width],
+                start=(a == 0),
+                stop=(a == PASSES - 1),
+            )
+
+        def first_half(s0, n, a):
             for g0, width in groups:
                 if s0 <= g0 < s0 + n:
                     e = g0 // C
                     if a == 0:
-                        acc[g0, h] = psum.tile([P, width], F32, name="bank")
-                    nc.tensor.matmul_mx(
-                        out=acc[g0, h][:],
-                        lhsT=w_sb[e][:, a, h * P:(h + 1) * P].bitcast(FP8X4),
-                        lhsT_scale=w_sc[:, e * PASSES + a, h * P:(h + 1) * P],
-                        rhs=x_codes[a][:, g0:g0 + width].bitcast(FP8X4),
-                        rhs_scale=x_sc[a][:, g0:g0 + width],
-                        start=(a == 0),
-                        stop=(a == PASSES - 1),
-                    )
-                    if a == PASSES - 1:
-                        if (g0, h) == (groups[-1][0], 0):
-                            nc.vector.tensor_scalar(y[h][:, g0:g0 + width], acc[g0, h][:], bias[:, h, e:e + 1], None, ADD)
-                        else:
-                            nc.scalar.activation(y[h][:, g0:g0 + width], acc[g0, h][:], IDENTITY, bias=bias[:, h, e:e + 1])
+                        acc[g0] = psum.tile([P, width], F32, name="bank")
+                    one_pass(acc[g0], g0, width, a, 0)
+                    if a == PASSES - 1 and e == E - 1:
+                        nc.vector.tensor_scalar(y[0][:, g0:g0 + width], acc[g0][:], bias[:, 0, e:e + 1], None, ADD)
+                    elif a == PASSES - 1:
+                        nc.scalar.activation(y[0][:, g0:g0 + width], acc[g0][:], IDENTITY, bias=bias[:, 0, e:e + 1])
+
+        def second_half(e):
+            bank = psum.tile([P, C], F32, name="bank")
+            for a in range(PASSES):
+                one_pass(bank, e * C, C, a, 1)
+            nc.scalar.activation(y[1][:, e * C:(e + 1) * C], bank[:], IDENTITY, bias=bias[:, 1, e:e + 1])
 
         waiting = []
         for i, piece in enumerate(PIECES):
-            made = gather(*piece)
+            rounded = gather(*piece)
             if i <= len(PIECES) - HELD:
-                for s0, n, a, rounded in waiting:
-                    quantize(s0, n, a, rounded)
-                    for h in range(HALVES):
-                        multiply(s0, n, a, h)
+                for s0, n, a, earlier in waiting:
+                    quantize(s0, n, a, earlier)
+                    first_half(s0, n, a)
+                    if (s0, a) == (0, PASSES - 1):
+                        for e in range(E // 2):
+                            second_half(e)
                 waiting = []
-            waiting += made
-        for s0, n, a, rounded in waiting:
-            quantize(s0, n, a, rounded)
-            multiply(s0, n, a, 0)
-        for s0, n, a, rounded in waiting:
-            multiply(s0, n, a, 1)
+            waiting.append(piece + (rounded,))
+        for s0, n, a, earlier in waiting:
+            quantize(s0, n, a, earlier)
+        for s0, n, a, earlier in waiting:
+            first_half(s0, n, a)
+        for e in range(E // 2, E):
+            second_half(e)
 
         back = [keep.tile([P, TOP, T], F32, name="back%d" % h) for h in range(HALVES)]
 
@@ -159,7 +163,7 @@ def tile_moe_pre_lin_bias_kernel(tc, xT, w_words, w_scales, b, gate, offs, pos1,
             nc.vector.tensor_copy(back[h][:, r, t0:t1], y[h][:].indirect(pos_sb[r][:, t0 // PER_COL:t1 // PER_COL]))
 
         def store(queue, h, t0, total):
-            queue.dma_start(out=out[h * P:(h + 1) * P, t0:t0 + UNIT], in_=total[:])
+            queue.dma_start(out=out[h * P:(h + 1) * P, t0:t0 + total.shape[1]], in_=total)
 
         def turn_and_add(turned, h, r, t0):
             for c0 in range(0, UNIT, P):
@@ -174,7 +178,7 @@ def tile_moe_pre_lin_bias_kernel(tc, xT, w_words, w_scales, b, gate, offs, pos1,
                 nc.tensor.transpose(upright[:, c0:c0 + P], summed[:, c0:c0 + P], ident[:])
             total = narrow.tile([P, UNIT], F32, name="total")
             nc.scalar.copy(out=total[:], in_=upright[:])
-            store(nc.scalar, h, t0, total)
+            store(nc.scalar, h, t0, total[:])
 
         for h, t0, t1 in ((0, 0, T), (1, 0, UNIT)):
             turned = {u: psum.tile([P, UNIT], F32, name="bank") for u in range(t0, t1, UNIT)}
@@ -191,6 +195,8 @@ def tile_moe_pre_lin_bias_kernel(tc, xT, w_words, w_scales, b, gate, offs, pos1,
             fetch(1, r, UNIT, T)
         nc.vector.tensor_tensor(two[:], back[1][:, 0, UNIT:], back[1][:, 1, UNIT:], ADD)
         fetch(1, TOP - 1, UNIT, T)
-        nc.vector.tensor_tensor(three[:], two[:], back[1][:, 2, UNIT:], ADD)
-        nc.vector.tensor_tensor(four[:], three[:], back[1][:, 3, UNIT:], ADD)
-        store(nc.sync, 1, UNIT, four)
+        for c0 in range(0, UNIT, P):
+            nc.vector.tensor_tensor(three[:, c0:c0 + P], two[:, c0:c0 + P], back[1][:, 2, UNIT + c0:UNIT + c0 + P], ADD)
+        for c0 in range(0, UNIT, P):
+            nc.vector.tensor_tensor(four[:, c0:c0 + P], three[:, c0:c0 + P], back[1][:, 3, UNIT + c0:UNIT + c0 + P], ADD)
+            store(nc.sync, 1, UNIT + c0, four[:, c0:c0 + P])

@@ -31,6 +31,7 @@ PIECES = [(0, 1024, 0), (0, 1024, 1), (0, 1024, 2), (1024, 1024, 0), (1024, 1024
           (1024, 512, 2), (1536, 256, 2), (1792, 128, 2), (1920, 128, 2)]
 HELD = 3
 UNIT = 256
+WHOLE = 2
 GATE_CUTS = [0, 128, 512, 1024, 2048]
 LINE = 4
 
@@ -183,7 +184,7 @@ def tile_moe_pre_lin_bias_kernel(tc, xT, w_words, w_scales, b, gate, offs, pos1,
         for h, t0, t1 in ((0, 0, T), (1, 0, UNIT)):
             turned = {u: psum.tile([P, UNIT], F32, name="bank") for u in range(t0, t1, UNIT)}
             for r in range(TOP):
-                fetch(h, r, t0, t1)
+                fetch(h, r, t0, T if r < WHOLE else t1)
                 for u in range(t0, t1, UNIT):
                     turn_and_add(turned[u], h, r, u)
             for u in range(t0, t1, UNIT):
@@ -191,8 +192,7 @@ def tile_moe_pre_lin_bias_kernel(tc, xT, w_words, w_scales, b, gate, offs, pos1,
         two = keep.tile([P, UNIT], F32, name="two")
         three = keep.tile([P, UNIT], F32, name="three")
         four = keep.tile([P, UNIT], F32, name="four")
-        for r in range(TOP - 1):
-            fetch(1, r, UNIT, T)
+        fetch(1, WHOLE, UNIT, T)
         nc.vector.tensor_tensor(two[:], back[1][:, 0, UNIT:], back[1][:, 1, UNIT:], ADD)
         fetch(1, TOP - 1, UNIT, T)
         for c0 in range(0, UNIT, P):

from contextlib import ExitStack

import concourse.mybir as mybir
from concourse.masks import make_identity

K, T, E, C, N = 1536, 512, 8, 256, 256
TOP = 4
S = E * C
P = 128
PACK = 4
PASSES = K // (P * PACK)
HALVES = N // P
WINDOW = 1032
PER_COL = 16

F32 = mybir.dt.float32
BF16 = mybir.dt.bfloat16
I32 = mybir.dt.int32
U32 = mybir.dt.uint32
U16 = mybir.dt.uint16
U8 = mybir.dt.uint8
FP8X4 = mybir.dt.float8_e4m3fn_x4
MULT = mybir.AluOpType.mult
ADD = mybir.AluOpType.add
IDENTITY = mybir.ActivationFunctionType.Identity

FLOPS = 2 * K * N * S
BYTES = 4 * K * T + E * K * N + E * K * N // 32 + 4 * N * E + 4 * S + 2 * P * (S + TOP * T) // PER_COL + 4 * N * T

PIECES = [(0, 1024, 0), (0, 1024, 1), (0, 1024, 2), (1024, 1024, 0), (1024, 1024, 1),
          (1024, 512, 2), (1536, 256, 2), (1792, 128, 2), (1920, 128, 2)]
HELD = 3
UNIT = 256
WHOLE = 2
GATE_CUTS = [0, 128, 512, 1024, 2048]
LINE = 4


def tile_moe_pre_lin_bias_kernel(tc, xT, w_words, w_scales, b, gate, offs, pos1, pos2, pos3, pos4, out):
    nc = tc.nc
    with ExitStack() as ctx:
        keep = ctx.enter_context(tc.tile_pool(name="keep", bufs=1))
        stage = ctx.enter_context(tc.tile_pool(name="stage", bufs=2))
        narrow = ctx.enter_context(tc.tile_pool(name="narrow", bufs=4))
        psum = ctx.enter_context(tc.psum_pool(name="psum", bufs=8))

        offs_sb = keep.tile([P, S // PER_COL], U16, name="offs_sb")
        pos_sb = [keep.tile([P, T // PER_COL], U16, name="pos%d" % r) for r in range(TOP)]
        rows = [[keep.tile([P, WINDOW], F32, name="rows%d_%d" % (a, j)) for j in range(PACK)] for a in range(PASSES)]
        gate_sb = keep.tile([P, S], F32, name="gate_sb")
        w_sb = [keep.tile([P, PASSES, N], U32, name="w%d" % e, align_bytes=64) for e in range(E)]
        w_sc = keep.tile([P, E * PASSES, N], U8, name="w_sc", align_bytes=64)
        bias = keep.tile([P, HALVES, E], F32, name="bias")
        x_codes = [keep.tile([P, S], U32, name="x_codes%d" % a, align_bytes=64) for a in range(PASSES)]
        x_sc = [keep.tile([P, S], U8, name="x_sc%d" % a, align_bytes=64) for a in range(PASSES)]
        y = [keep.tile([P, S], F32, name="y%d" % h) for h in range(HALVES)]

        ident = keep.tile([P, P], F32, name="ident")
        make_identity(nc, ident[:])
        nc.vector.memset(w_sc[:].rearrange("p g n -> p (g n)").bitcast(I32), 0)

        def load_rows(a, j):
            src = xT[a * P * PACK:(a + 1) * P * PACK, :].rearrange("(p j) t -> p j t", j=PACK)
            nc.sync.dma_start(out=rows[a][j][:, :T], in_=src[:, j, :])

        def load_gate(s0, s1):
            nc.sync.dma_start(out=gate_sb[:, s0:s1], in_=gate[0:P, s0:s1])

        def load_weights(e):
            nc.sync.dma_start(out=w_sb[e][:].bitcast(I32), in_=w_words[e].rearrange("a p n r -> p a (n r)").bitcast(I32))

        nc.sync.dma_start(offs_sb[:], offs)
        load_rows(0, 0)
        for g0, g1 in zip(GATE_CUTS[:3], GATE_CUTS[1:4]):
            load_gate(g0, g1)
        for a in range(PASSES):
            for j in range(PACK):
                if (a, j) != (0, 0):
                    load_rows(a, j)
        load_gate(GATE_CUTS[3], S)
        scale_rows = w_scales.rearrange("e a q n -> q (e a) n").bitcast(I32)
        for quad in range(4):
            nc.sync.dma_start(out=w_sc[32 * quad:32 * quad + 4, :, :].bitcast(I32), in_=scale_rows[4 * quad:4 * quad + 4, :, :])
        nc.sync.dma_start(out=bias[:], in_=b.rearrange("(h p) e -> p h e", p=P))
        for e in range(E):
            load_weights(e)
        for r, pos in enumerate((pos1, pos2, pos3, pos4)):
            nc.sync.dma_start(pos_sb[r][:], pos)

        groups = [(e * C, C) for e in range(E - 1)] + [(S - C, C // 2), (S - C // 2, C // 2)]
        acc = {}

        def gather(s0, n, a):
            picked = stage.tile([P, PACK, n], F32, name="picked")
            for j in range(PACK):
                cuts = GATE_CUTS[:4] if (s0, a, j) == (0, 0, 0) else [0, n]
                for c0, c1 in zip(cuts, cuts[1:]):
                    window = rows[a][j][:].indirect(offs_sb[:, (s0 + c0) // PER_COL:(s0 + c1) // PER_COL])
                    nc.vector.tensor_tensor(picked[:, j, c0:c1], window, gate_sb[:, s0 + c0:s0 + c1], MULT)
            rounded = narrow.tile([P, n, PACK], BF16, name="rounded", align_bytes=64)
            nc.scalar.copy(out=rounded[:].rearrange("p (c i) j -> p c j i", i=LINE),
                           in_=picked[:].rearrange("p j (c i) -> p c j i", i=LINE))
            return rounded

        def quantize(s0, n, a, rounded):
            nc.vector.quantize_mx(
                out=x_codes[a][:, s0:s0 + n].bitcast(FP8X4),
                scales=x_sc[a][:, s0:s0 + n],
                in_=rounded[:].rearrange("p c j -> p (c j)"),
            )

        def one_pass(bank, g0, width, a, h):
            e = g0 // C
            nc.tensor.matmul_mx(
                out=bank[:],
                lhsT=w_sb[e][:, a, h * P:(h + 1) * P].bitcast(FP8X4),
                lhsT_scale=w_sc[:, e * PASSES + a, h * P:(h + 1) * P],
                rhs=x_codes[a][:, g0:g0 + width].bitcast(FP8X4),
                rhs_scale=x_sc[a][:, g0:g0 + width],
                start=(a == 0),
                stop=(a == PASSES - 1),
            )

        def first_half(s0, n, a):
            for g0, width in groups:
                if s0 <= g0 < s0 + n:
                    e = g0 // C
                    if a == 0:
                        acc[g0] = psum.tile([P, width], F32, name="bank")
                    one_pass(acc[g0], g0, width, a, 0)
                    if a == PASSES - 1 and e == E - 1:
                        nc.vector.tensor_scalar(y[0][:, g0:g0 + width], acc[g0][:], bias[:, 0, e:e + 1], None, ADD)
                    elif a == PASSES - 1:
                        nc.scalar.activation(y[0][:, g0:g0 + width], acc[g0][:], IDENTITY, bias=bias[:, 0, e:e + 1])

        def second_half(e):
            bank = psum.tile([P, C], F32, name="bank")
            for a in range(PASSES):
                one_pass(bank, e * C, C, a, 1)
            nc.scalar.activation(y[1][:, e * C:(e + 1) * C], bank[:], IDENTITY, bias=bias[:, 1, e:e + 1])

        waiting = []
        for i, piece in enumerate(PIECES):
            rounded = gather(*piece)
            if i <= len(PIECES) - HELD:
                for s0, n, a, earlier in waiting:
                    quantize(s0, n, a, earlier)
                    first_half(s0, n, a)
                    if (s0, a) == (0, PASSES - 1):
                        for e in range(E // 2):
                            second_half(e)
                waiting = []
            waiting.append(piece + (rounded,))
        for s0, n, a, earlier in waiting:
            quantize(s0, n, a, earlier)
        for s0, n, a, earlier in waiting:
            first_half(s0, n, a)
        for e in range(E // 2, E):
            second_half(e)

        back = [keep.tile([P, TOP, T], F32, name="back%d" % h) for h in range(HALVES)]

        def fetch(h, r, t0, t1):
            nc.vector.tensor_copy(back[h][:, r, t0:t1], y[h][:].indirect(pos_sb[r][:, t0 // PER_COL:t1 // PER_COL]))

        def store(queue, h, t0, total):
            queue.dma_start(out=out[h * P:(h + 1) * P, t0:t0 + total.shape[1]], in_=total)

        def turn_and_add(turned, h, r, t0):
            for c0 in range(0, UNIT, P):
                nc.tensor.matmul(turned[:, c0:c0 + P], lhsT=back[h][:, r, t0 + c0:t0 + c0 + P], rhs=ident[:],
                                 start=(r == 0 and c0 == 0), stop=(r == TOP - 1 and c0 == UNIT - P), is_transpose=True)

        def turn_back(turned, h, t0):
            summed = narrow.tile([P, UNIT], F32, name="summed")
            nc.scalar.copy(out=summed[:], in_=turned[:])
            upright = psum.tile([P, UNIT], F32, name="bank")
            for c0 in range(0, UNIT, P):
                nc.tensor.transpose(upright[:, c0:c0 + P], summed[:, c0:c0 + P], ident[:])
            total = narrow.tile([P, UNIT], F32, name="total")
            nc.scalar.copy(out=total[:], in_=upright[:])
            store(nc.scalar, h, t0, total[:])

        for h, t0, t1 in ((0, 0, T), (1, 0, UNIT)):
            turned = {u: psum.tile([P, UNIT], F32, name="bank") for u in range(t0, t1, UNIT)}
            for r in range(TOP):
                fetch(h, r, t0, T if r < WHOLE else t1)
                for u in range(t0, t1, UNIT):
                    turn_and_add(turned[u], h, r, u)
            for u in range(t0, t1, UNIT):
                turn_back(turned[u], h, u)
        two = keep.tile([P, UNIT], F32, name="two")
        three = keep.tile([P, UNIT], F32, name="three")
        four = keep.tile([P, UNIT], F32, name="four")
        fetch(1, WHOLE, UNIT, T)
        nc.vector.tensor_tensor(two[:], back[1][:, 0, UNIT:], back[1][:, 1, UNIT:], ADD)
        fetch(1, TOP - 1, UNIT, T)
        for c0 in range(0, UNIT, P):
            nc.vector.tensor_tensor(three[:, c0:c0 + P], two[:, c0:c0 + P], back[1][:, 2, UNIT + c0:UNIT + c0 + P], ADD)
        for c0 in range(0, UNIT, P):
            nc.vector.tensor_tensor(four[:, c0:c0 + P], three[:, c0:c0 + P], back[1][:, 3, UNIT + c0:UNIT + c0 + P], ADD)
            store(nc.sync, 1, UNIT + c0, four[:, c0:c0 + P])
